import numpy as np
import ml_dtypes


def mxq(x, axis, fmt="e4m3"):
    dtype, down = {"e4m3": (ml_dtypes.float8_e4m3fn, 7), "e5m2": (ml_dtypes.float8_e5m2, 14)}[fmt]
    v = np.moveaxis(np.asarray(x, np.float32).astype(ml_dtypes.bfloat16).astype(np.float64), axis, -1)
    blocks = v.reshape(v.shape[:-1] + (-1, 32))
    amax = np.abs(blocks).max(-1, keepdims=True)
    byte = np.maximum(np.where(amax > 0, np.frexp(amax)[1] - 1 + 127, 0) - down, 1)
    scale = np.exp2(byte - 127.0)
    codes = (blocks / scale).astype(np.float32).astype(dtype).astype(np.float64)
    return np.moveaxis((codes * scale).reshape(v.shape), -1, axis)


WIDE = False


def mx_kscale(k):
    if not WIDE:
        return np.ones(k)
    levels = np.array([10, -10, 5, -5, 0])
    if k % 512:
        return np.exp2(np.random.permutation(np.resize(levels, k // 32))).repeat(32)
    a = np.empty((k // 512, 16))
    for p in range(k // 512):
        a[p, :8] = np.random.permutation(np.resize(levels, 8))
        for g in range(8):
            far = levels[np.abs(levels - a[p, g]) >= 10]
            a[p, g + 8] = far[np.random.randint(len(far))]
    return np.exp2(a.ravel()).repeat(32)


def f64(x):
    return np.asarray(x).astype(np.float64)


def striped(idx):
    return np.tile(np.asarray(idx).reshape(-1, 16).T, (8, 1)).astype(np.uint16)


def unstriped(offs):
    return offs[:16].T.reshape(-1).astype(np.int64)


E2M1 = np.array([0.0, 0.5, 1.0, 1.5, 2.0, 3.0, 4.0, 6.0, -0.0, -0.5, -1.0, -1.5, -2.0, -3.0, -4.0, -6.0])


def pack_weight(w, fmt):
    k, n = w.shape
    w = f64(np.asarray(w, np.float32).astype(ml_dtypes.bfloat16)).reshape(k // 32, 32, n)
    amax = np.abs(w).max(1)
    if fmt == "e4m3":
        byte = np.frexp(amax)[1] - 1 + 127 - 7
    else:
        mant, ex = np.frexp(amax / 6.0)
        byte = np.where(mant > 0.5, ex, ex - 1) + 127
    byte = np.clip(np.where(amax > 0, byte, 1), 1, 254)
    scaled = (w * np.exp2(127.0 - byte)[:, None, :]).reshape(k, n).astype(np.float32)
    by_word = np.ascontiguousarray(scaled.reshape(k // 512, 128, 4, n).transpose(0, 1, 3, 2))
    if fmt == "e4m3":
        words = by_word.astype(ml_dtypes.float8_e4m3fn).view(np.uint8)
    else:
        c = by_word.astype(ml_dtypes.float4_e2m1fn).view(np.uint8) & 0xF
        words = (c[..., 0::2] | (c[..., 1::2] << 4)).reshape(k // 512, 128, 2 * n)
    return np.ascontiguousarray(words), np.ascontiguousarray(byte.astype(np.uint8).reshape(k // 512, 16, n))


def unpack_weight(words, scales, fmt):
    g, _, n = scales.shape
    words = np.ascontiguousarray(words).reshape(g, 128, n, -1)
    if fmt == "e4m3":
        vals = words.view(ml_dtypes.float8_e4m3fn).astype(np.float64)
    else:
        nib = np.empty((g, 128, n, 4), np.uint8)
        nib[..., 0::2] = words & 0xF
        nib[..., 1::2] = words >> 4
        vals = E2M1[nib]
    vals = vals * np.repeat(np.exp2(scales.astype(np.float64) - 127.0), 8, axis=1)[..., None]
    return vals.transpose(0, 1, 3, 2).reshape(g * 512, n)


def sigmoid(v):
    return 1.0 / (1.0 + np.exp(-v))


K, R, F, T, J = 512, 128, 512, 2048, 512


def setup_inputs():
    n = np.random.standard_normal
    idx = np.random.permutation(T)[:J]
    idx2 = np.random.permutation(T)[:J]
    fk = mx_kscale(K)
    ff = mx_kscale(F)
    tabp = pack_weight(n((K, T)) / fk[:, None], "e2m1")
    tab2p = pack_weight(n((K, T)) / fk[:, None], "e2m1")
    dtabp = pack_weight(n((K, T)) / fk[:, None], "e2m1")
    return {
        "tab_words": tabp[0],
        "tab_scales": tabp[1],
        "w1": (n((K, R)) * 1 / np.sqrt(K) * fk[:, None]).astype(np.float32),
        "tab2_words": tab2p[0],
        "tab2_scales": tab2p[1],
        "w2": (n((K, R)) * 1 / np.sqrt(K) * fk[:, None]).astype(np.float32),
        "bias": (np.random.uniform(-0.5, 0.5, (R, 1))).astype(np.float32),
        "wo": (n((F, R)) * 1 / np.sqrt(F) * ff[:, None]).astype(np.float32),
        "dy": (n((F, J)) / ff[:, None]).astype(np.float32),
        "dtab_words": dtabp[0],
        "dtab_scales": dtabp[1],
        "og": (np.random.uniform(0.7, 2.0, (R, 1))).astype(np.float32),
        "base": (0.3 * n((R, J))).astype(np.float32),
        "offs": striped(idx),
        "offs2": striped(idx2),
    }


def reference(tab_words, tab_scales, w1, tab2_words, tab2_scales, w2, bias, wo, dy, dtab_words, dtab_scales, og, base, offs, offs2):
    idx = unstriped(offs)
    idx2 = unstriped(offs2)
    tabu = unpack_weight(tab_words, tab_scales, "e2m1")
    tab2u = unpack_weight(tab2_words, tab2_scales, "e2m1")
    dtabu = unpack_weight(dtab_words, dtab_scales, "e2m1")
    w1q = mxq(f64(w1), 0, "e4m3")
    tabidxg = tabu[:, idx]
    a = w1q.T @ tabidxg
    dtabidxg = dtabu[:, idx]
    ta = w1q.T @ dtabidxg
    w2q = mxq(f64(w2), 0, "e4m3")
    tab2idx2g = tab2u[:, idx2]
    b = w2q.T @ tab2idx2g
    h1 = np.tanh(a)
    gt = sigmoid(b + f64(bias))
    woq = mxq(f64(wo), 0, "e4m3")
    dyq = mxq(f64(dy), 0, "e4m3")
    c0 = woq.T @ dyq
    xh1 = ta * (1.0 - np.square(h1))
    xdgt = xh1 * c0
    xdb = xdgt * gt * (1.0 - gt)
    y = xdb * f64(og) + f64(base)
    return y

@@ -1,0 +1,166 @@
+from contextlib import ExitStack
+
+import concourse.mybir as mybir
+
+K, R, F, T, J = 512, 128, 512, 2048, 512
+FLOPS = 4 * 2 * K * R * J
+
+F32 = mybir.dt.float32
+BF16 = mybir.dt.bfloat16
+I32 = mybir.dt.int32
+U32 = mybir.dt.uint32
+U16 = mybir.dt.uint16
+U8 = mybir.dt.uint8
+FP8X4 = mybir.dt.float8_e4m3fn_x4
+FP4X4 = mybir.dt.float4_e2m1fn_x4
+ALU = mybir.AluOpType
+ACT = mybir.ActivationFunctionType
+
+P = 128
+PACK = 4
+HALF = J // 2
+LIST_COLS = J // 16
+
+
+def tile_attend_hvtwotables_kernel(tc, tab_words, tab_scales, w1, tab2_words, tab2_scales, w2, bias, wo, dy,
+                                    dtab_words, dtab_scales, og, base, offs, offs2, out):
+    nc = tc.nc
+    with ExitStack() as ctx:
+        sb = ctx.enter_context(tc.tile_pool(name="sb", bufs=1))
+        ps = ctx.enter_context(tc.psum_pool(name="ps", bufs=1))
+
+        def zeroed_scale_table(name):
+            table = sb.tile([P, T], U8, name=name, align_bytes=64)
+            nc.vector.memset(table[:].bitcast(I32), 0)
+            return table
+
+        def load_scale_rows(table, scales):
+            rows = scales[0].bitcast(I32)
+            for r in range(4):
+                nc.sync.dma_start(table[:].bitcast(I32)[r:P:32, :], rows[r:16:4, :])
+
+        def load_words(name, words):
+            table = sb.tile([P, T], U16, name=name, tag=name, align_bytes=64)
+            nc.sync.dma_start(table[:].bitcast(I32), words[0].bitcast(I32))
+            return table
+
+        def load_list(name, src):
+            lst = sb.tile([P, LIST_COLS], U16, name=name)
+            nc.sync.dma_start(lst[:], src)
+            return lst
+
+        def load_rows(name, src, c0, width):
+            raw = sb.tile([P, PACK, width], F32, name=name, tag=name, align_bytes=64)
+            nc.sync.dma_start(raw[:], src.rearrange("(p t) c -> p t c", t=PACK)[:, :, c0:c0 + width])
+            return raw
+
+        def interleave(grouped, raw):
+            nc.scalar.activation(
+                grouped.rearrange("p (c i) t -> p c t i", i=4),
+                raw[:].rearrange("p t (c i) -> p c t i", i=4),
+                ACT.Copy,
+            )
+
+        def grouped_tile(name, width):
+            return sb.tile([P, width, PACK], BF16, name=name, align_bytes=64)
+
+        def quantise(name, grouped, tag=None):
+            width = grouped.shape[1]
+            codes = sb.tile([P, width], U32, name=name + "_codes", tag=tag or name + "_codes", align_bytes=64)
+            scales = sb.tile([P, width], U8, name=name + "_scales", align_bytes=64)
+            nc.vector.quantize_mx(codes[:].bitcast(FP8X4), scales[:], grouped[:].rearrange("p c t -> p (c t)"))
+            return codes, scales
+
+        def gather(name, table, offsets, dtype):
+            picked = sb.tile([P, offsets.shape[1] * 16], dtype, name=name, align_bytes=64)
+            nc.vector.tensor_copy(picked[:], table[:].indirect(offsets))
+            return picked
+
+        def product(acc, weights, codes, scales):
+            nc.tensor.matmul_mx(acc, lhsT=weights[0][:].bitcast(FP8X4), lhsT_scale=weights[1][:],
+                                rhs=codes, rhs_scale=scales, start=True, stop=True)
+
+        tab_s = zeroed_scale_table("tab_s")
+        tab2_s = zeroed_scale_table("tab2_s")
+        dtab_s = zeroed_scale_table("dtab_s")
+
+        bias_col = sb.tile([P, 1], F32, name="bias_col")
+        og_col = sb.tile([P, 1], F32, name="og_col")
+        nc.gpsimd.dma_start(bias_col[:], bias)
+        nc.gpsimd.dma_start(og_col[:], og)
+        half_bias = sb.tile([P, 1], F32, name="half_bias")
+        nc.gpsimd.tensor_scalar(half_bias[:], bias_col[:], 0.5, 0.0, ALU.mult, ALU.add)
+
+        w1_raw = load_rows("w1_raw", w1, 0, R)
+        idx = load_list("idx", offs)
+        load_scale_rows(tab_s, tab_scales)
+        tab_w = load_words("tab_w", tab_words)
+        w2_raw = load_rows("w2_raw", w2, 0, R)
+        idx2 = load_list("idx2", offs2)
+        load_scale_rows(tab2_s, tab2_scales)
+        dy_raw0 = load_rows("dy_raw0", dy, 0, HALF)
+        tab2_w = load_words("tab2_w", tab2_words)
+        wo_raw = load_rows("wo_raw", wo, 0, R)
+        load_scale_rows(dtab_s, dtab_scales)
+        dy_raw1 = load_rows("dy_raw1", dy, HALF, HALF)
+        dtab_w = load_words("dtab_w", dtab_words)
+        base_sb = sb.tile([P, J], F32, name="base_sb")
+        nc.sync.dma_start(base_sb[:], base)
+
+        a_ps = ps.tile([P, J], F32, name="a_ps")
+        b_ps = ps.tile([P, J], F32, name="b_ps")
+        c_ps = ps.tile([P, J], F32, name="c_ps")
+        ta_ps = [ps.tile([P, HALF], F32, name="ta_ps%d" % h) for h in range(2)]
+        halves = [slice(h * HALF, (h + 1) * HALF) for h in range(2)]
+
+        w1_g = grouped_tile("w1_g", R)
+        w2_g = grouped_tile("w2_g", R)
+        wo_g = grouped_tile("wo_g", R)
+        dy_g = grouped_tile("dy_g", J)
+
+        interleave(w1_g[:], w1_raw)
+        tab_sg = gather("tab_sg", tab_s, idx[:], U8)
+        w1_q = quantise("w1_q", w1_g)
+        tab_wg = gather("tab_wg", tab_w, idx[:], U16)
+        product(a_ps[:], w1_q, tab_wg[:].bitcast(FP4X4), tab_sg[:])
+
+        interleave(w2_g[:], w2_raw)
+        tab2_sg = gather("tab2_sg", tab2_s, idx2[:], U8)
+        w2_q = quantise("w2_q", w2_g)
+        interleave(dy_g[:, halves[0], :], dy_raw0)
+        tab2_wg = gather("tab2_wg", tab2_w, idx2[:], U16)
+        product(b_ps[:], w2_q, tab2_wg[:].bitcast(FP4X4), tab2_sg[:])
+
+        h1 = sb.tile([P, J], F32, name="h1", tag="dy_raw0", align_bytes=64)
+        nc.scalar.activation(h1[:], a_ps[:], ACT.Tanh)
+        h1_sq = sb.tile([P, J], F32, name="h1_sq")
+        nc.scalar.activation(h1_sq[:], h1[:], ACT.Square)
+
+        interleave(wo_g[:], wo_raw)
+        interleave(dy_g[:, halves[1], :], dy_raw1)
+        th = sb.tile([P, J], F32, name="th", tag="dy_raw1", align_bytes=64)
+        nc.scalar.activation(th[:], b_ps[:], ACT.Tanh, bias=half_bias[:], scale=0.5)
+        th_sq = sb.tile([P, J], F32, name="th_sq")
+        nc.scalar.activation(th_sq[:], th[:], ACT.Square, scale=0.5)
+
+        dtab_sg = gather("dtab_sg", dtab_s, idx[:], U8)
+        wo_q = quantise("wo_q", wo_g)
+        dtab_wg = gather("dtab_wg", dtab_w, idx[:], U16)
+        for h in range(2):
+            product(ta_ps[h][:], w1_q, dtab_wg[:, halves[h]].bitcast(FP4X4), dtab_sg[:, halves[h]])
+        dy_q = quantise("dy_q", dy_g, tag="dtab_w")
+        product(c_ps[:], wo_q, dy_q[0][:].bitcast(FP8X4), dy_q[1][:])
+
+        m1 = [sb.tile([P, HALF], F32, name="m1_%d" % h) for h in range(2)]
+        m2 = [sb.tile([P, HALF], F32, name="m2_%d" % h) for h in range(2)]
+        m3 = [sb.tile([P, HALF], F32, name="m3_%d" % h) for h in range(2)]
+        res = [sb.tile([P, HALF], F32, name="res_%d" % h) for h in range(2)]
+        for h in range(2):
+            nc.vector.scalar_tensor_tensor(m1[h][:], h1_sq[:, halves[h]], 1.0, ta_ps[h][:], ALU.subtract, ALU.mult)
+        for h in range(2):
+            nc.vector.scalar_tensor_tensor(m2[h][:], th_sq[:, halves[h]], 0.25, m1[h][:], ALU.subtract, ALU.mult)
+        for h in range(2):
+            nc.vector.tensor_tensor(m3[h][:], m2[h][:], c_ps[:, halves[h]], ALU.mult)
+        for h in range(2):
+            nc.vector.scalar_tensor_tensor(res[h][:], m3[h][:], og_col[:], base_sb[:, halves[h]], ALU.mult, ALU.add)
+            nc.sync.dma_start(out[:, halves[h]], res[h][:])

@@ -30,7 +30,7 @@ def tile_attend_hvtwotables_kernel(tc, tab_words, tab_scales, w1, tab2_words, ta
         ps = ctx.enter_context(tc.psum_pool(name="ps", bufs=1))
 
         def zeroed_scale_table(name):
-            table = sb.tile([P, T], U8, name=name, align_bytes=64)
+            table = sb.tile([P, T], U8, name=name, tag=name, align_bytes=64)
             nc.vector.memset(table[:].bitcast(I32), 0)
             return table
 
@@ -54,15 +54,14 @@ def tile_attend_hvtwotables_kernel(tc, tab_words, tab_scales, w1, tab2_words, ta
             nc.sync.dma_start(raw[:], src.rearrange("(p t) c -> p t c", t=PACK)[:, :, c0:c0 + width])
             return raw
 
-        def interleave(grouped, raw):
+        def interleave(name, raw, tag=None):
+            grouped = sb.tile([P, raw.shape[2], PACK], BF16, name=name, tag=tag or name, align_bytes=64)
             nc.scalar.activation(
-                grouped.rearrange("p (c i) t -> p c t i", i=4),
+                grouped[:].rearrange("p (c i) t -> p c t i", i=4),
                 raw[:].rearrange("p t (c i) -> p c t i", i=4),
                 ACT.Copy,
             )
-
-        def grouped_tile(name, width):
-            return sb.tile([P, width, PACK], BF16, name=name, align_bytes=64)
+            return grouped
 
         def quantise(name, grouped, tag=None):
             width = grouped.shape[1]
@@ -71,8 +70,8 @@ def tile_attend_hvtwotables_kernel(tc, tab_words, tab_scales, w1, tab2_words, ta
             nc.vector.quantize_mx(codes[:].bitcast(FP8X4), scales[:], grouped[:].rearrange("p c t -> p (c t)"))
             return codes, scales
 
-        def gather(name, table, offsets, dtype):
-            picked = sb.tile([P, offsets.shape[1] * 16], dtype, name=name, align_bytes=64)
+        def gather(name, table, offsets, dtype, tag=None):
+            picked = sb.tile([P, offsets.shape[1] * 16], dtype, name=name, tag=tag or name, align_bytes=64)
             nc.vector.tensor_copy(picked[:], table[:].indirect(offsets))
             return picked
 
@@ -86,81 +85,76 @@ def tile_attend_hvtwotables_kernel(tc, tab_words, tab_scales, w1, tab2_words, ta
 
         bias_col = sb.tile([P, 1], F32, name="bias_col")
         og_col = sb.tile([P, 1], F32, name="og_col")
-        nc.gpsimd.dma_start(bias_col[:], bias)
-        nc.gpsimd.dma_start(og_col[:], og)
-        half_bias = sb.tile([P, 1], F32, name="half_bias")
-        nc.gpsimd.tensor_scalar(half_bias[:], bias_col[:], 0.5, 0.0, ALU.mult, ALU.add)
+        base_sb = sb.tile([P, J], F32, name="base_sb")
 
-        w1_raw = load_rows("w1_raw", w1, 0, R)
+        tab_w = load_words("tab_w", tab_words)
         idx = load_list("idx", offs)
         load_scale_rows(tab_s, tab_scales)
-        tab_w = load_words("tab_w", tab_words)
-        w2_raw = load_rows("w2_raw", w2, 0, R)
+        w1_raw = load_rows("w1_raw", w1, 0, R)
+        tab2_w = load_words("tab2_w", tab2_words)
         idx2 = load_list("idx2", offs2)
         load_scale_rows(tab2_s, tab2_scales)
+        w2_raw = load_rows("w2_raw", w2, 0, R)
         dy_raw0 = load_rows("dy_raw0", dy, 0, HALF)
-        tab2_w = load_words("tab2_w", tab2_words)
-        wo_raw = load_rows("wo_raw", wo, 0, R)
         load_scale_rows(dtab_s, dtab_scales)
-        dy_raw1 = load_rows("dy_raw1", dy, HALF, HALF)
         dtab_w = load_words("dtab_w", dtab_words)
-        base_sb = sb.tile([P, J], F32, name="base_sb")
+        nc.sync.dma_start(bias_col[:], bias)
+        wo_raw = load_rows("wo_raw", wo, 0, R)
+        dy_raw1 = load_rows("dy_raw1", dy, HALF, HALF)
+        nc.sync.dma_start(og_col[:], og)
         nc.sync.dma_start(base_sb[:], base)
 
         a_ps = ps.tile([P, J], F32, name="a_ps")
         b_ps = ps.tile([P, J], F32, name="b_ps")
-        c_ps = ps.tile([P, J], F32, name="c_ps")
+        c_ps = [ps.tile([P, HALF], F32, name="c_ps%d" % h) for h in range(2)]
         ta_ps = [ps.tile([P, HALF], F32, name="ta_ps%d" % h) for h in range(2)]
         halves = [slice(h * HALF, (h + 1) * HALF) for h in range(2)]
 
-        w1_g = grouped_tile("w1_g", R)
-        w2_g = grouped_tile("w2_g", R)
-        wo_g = grouped_tile("wo_g", R)
-        dy_g = grouped_tile("dy_g", J)
-
-        interleave(w1_g[:], w1_raw)
-        tab_sg = gather("tab_sg", tab_s, idx[:], U8)
-        w1_q = quantise("w1_q", w1_g)
         tab_wg = gather("tab_wg", tab_w, idx[:], U16)
+        tab_sg = gather("tab_sg", tab_s, idx[:], U8)
+        w1_q = quantise("w1_q", interleave("w1_g", w1_raw))
         product(a_ps[:], w1_q, tab_wg[:].bitcast(FP4X4), tab_sg[:])
 
-        interleave(w2_g[:], w2_raw)
+        tab2_wg = gather("tab2_wg", tab2_w, idx2[:], U16, tag="w1_raw")
         tab2_sg = gather("tab2_sg", tab2_s, idx2[:], U8)
-        w2_q = quantise("w2_q", w2_g)
-        interleave(dy_g[:, halves[0], :], dy_raw0)
-        tab2_wg = gather("tab2_wg", tab2_w, idx2[:], U16)
+        w2_q = quantise("w2_q", interleave("w2_g", w2_raw))
         product(b_ps[:], w2_q, tab2_wg[:].bitcast(FP4X4), tab2_sg[:])
 
-        h1 = sb.tile([P, J], F32, name="h1", tag="dy_raw0", align_bytes=64)
+        h1 = sb.tile([P, J], F32, name="h1")
         nc.scalar.activation(h1[:], a_ps[:], ACT.Tanh)
         h1_sq = sb.tile([P, J], F32, name="h1_sq")
         nc.scalar.activation(h1_sq[:], h1[:], ACT.Square)
 
-        interleave(wo_g[:], wo_raw)
-        interleave(dy_g[:, halves[1], :], dy_raw1)
-        th = sb.tile([P, J], F32, name="th", tag="dy_raw1", align_bytes=64)
+        dy_g0 = interleave("dy_g0", dy_raw0)
+        half_bias = sb.tile([P, 1], F32, name="half_bias")
+        nc.scalar.activation(half_bias[:], bias_col[:], ACT.Copy, scale=0.5)
+        th = sb.tile([P, J], F32, name="th", tag="dy_raw0", align_bytes=64)
         nc.scalar.activation(th[:], b_ps[:], ACT.Tanh, bias=half_bias[:], scale=0.5)
         th_sq = sb.tile([P, J], F32, name="th_sq")
         nc.scalar.activation(th_sq[:], th[:], ACT.Square, scale=0.5)
+        wo_g = interleave("wo_g", wo_raw, tag="dy_raw0")
+        dy_g1 = interleave("dy_g1", dy_raw1)
 
-        dtab_sg = gather("dtab_sg", dtab_s, idx[:], U8)
+        dtab_sg = gather("dtab_sg", dtab_s, idx[:], U8, tag="w2_raw")
+        for h in range(2):
+            dtab_wg = gather("dtab_wg%d" % h, dtab_w, idx[:, h * LIST_COLS // 2:(h + 1) * LIST_COLS // 2], U16)
+            product(ta_ps[h][:], w1_q, dtab_wg[:].bitcast(FP4X4), dtab_sg[:, halves[h]])
+
+        dy_q0 = quantise("dy_q0", dy_g0, tag="dtab_wg0")
+        m1 = sb.tile([P, J], F32, name="m1")
+        for h in range(2):
+            nc.vector.scalar_tensor_tensor(m1[:, halves[h]], h1_sq[:, halves[h]], 1.0, ta_ps[h][:], ALU.subtract, ALU.mult)
         wo_q = quantise("wo_q", wo_g)
-        dtab_wg = gather("dtab_wg", dtab_w, idx[:], U16)
+        product(c_ps[0][:], wo_q, dy_q0[0][:].bitcast(FP8X4), dy_q0[1][:])
+        m2 = sb.tile([P, J], F32, name="m2", tag="wo_raw", align_bytes=64)
         for h in range(2):
-            product(ta_ps[h][:], w1_q, dtab_wg[:, halves[h]].bitcast(FP4X4), dtab_sg[:, halves[h]])
-        dy_q = quantise("dy_q", dy_g, tag="dtab_w")
-        product(c_ps[:], wo_q, dy_q[0][:].bitcast(FP8X4), dy_q[1][:])
-
-        m1 = [sb.tile([P, HALF], F32, name="m1_%d" % h) for h in range(2)]
-        m2 = [sb.tile([P, HALF], F32, name="m2_%d" % h) for h in range(2)]
-        m3 = [sb.tile([P, HALF], F32, name="m3_%d" % h) for h in range(2)]
-        res = [sb.tile([P, HALF], F32, name="res_%d" % h) for h in range(2)]
+            nc.vector.scalar_tensor_tensor(m2[:, halves[h]], th_sq[:, halves[h]], 0.25, m1[:, halves[h]], ALU.subtract, ALU.mult)
+        dy_q1 = quantise("dy_q1", dy_g1)
+        product(c_ps[1][:], wo_q, dy_q1[0][:].bitcast(FP8X4), dy_q1[1][:])
+        m3 = sb.tile([P, J], F32, name="m3", tag="dy_raw1", align_bytes=64)
         for h in range(2):
-            nc.vector.scalar_tensor_tensor(m1[h][:], h1_sq[:, halves[h]], 1.0, ta_ps[h][:], ALU.subtract, ALU.mult)
+            nc.vector.tensor_tensor(m3[:, halves[h]], m2[:, halves[h]], c_ps[h][:], ALU.mult)
+        res = sb.tile([P, J], F32, name="res", tag="dy_q1_codes", align_bytes=64)
         for h in range(2):
-            nc.vector.scalar_tensor_tensor(m2[h][:], th_sq[:, halves[h]], 0.25, m1[h][:], ALU.subtract, ALU.mult)
-        for h in range(2):
-            nc.vector.tensor_tensor(m3[h][:], m2[h][:], c_ps[:, halves[h]], ALU.mult)
-        for h in range(2):
-            nc.vector.scalar_tensor_tensor(res[h][:], m3[h][:], og_col[:], base_sb[:, halves[h]], ALU.mult, ALU.add)
-            nc.sync.dma_start(out[:, halves[h]], res[h][:])
+            nc.vector.scalar_tensor_tensor(res[:, halves[h]], m3[:, halves[h]], og_col[:], base_sb[:, halves[h]], ALU.mult, ALU.add)
+            nc.sync.dma_start(out[:, halves[h]], res[:, halves[h]])

@@ -126,14 +126,14 @@ def tile_attend_hvtwotables_kernel(tc, tab_words, tab_scales, w1, tab2_words, ta
         nc.scalar.activation(h1_sq[:], h1[:], ACT.Square)
 
         dy_g0 = interleave("dy_g0", dy_raw0)
+        wo_g = interleave("wo_g", wo_raw)
         half_bias = sb.tile([P, 1], F32, name="half_bias")
         nc.scalar.activation(half_bias[:], bias_col[:], ACT.Copy, scale=0.5)
-        th = sb.tile([P, J], F32, name="th", tag="dy_raw0", align_bytes=64)
+        th = sb.tile([P, J], F32, name="th", tag="wo_raw", align_bytes=64)
         nc.scalar.activation(th[:], b_ps[:], ACT.Tanh, bias=half_bias[:], scale=0.5)
-        th_sq = sb.tile([P, J], F32, name="th_sq")
-        nc.scalar.activation(th_sq[:], th[:], ACT.Square, scale=0.5)
-        wo_g = interleave("wo_g", wo_raw, tag="dy_raw0")
         dy_g1 = interleave("dy_g1", dy_raw1)
+        th_sq = sb.tile([P, J], F32, name="th_sq", tag="dy_raw1", align_bytes=64)
+        nc.scalar.activation(th_sq[:], th[:], ACT.Square, scale=0.5)
 
         dtab_sg = gather("dtab_sg", dtab_s, idx[:], U8, tag="w2_raw")
         for h in range(2):
@@ -144,17 +144,17 @@ def tile_attend_hvtwotables_kernel(tc, tab_words, tab_scales, w1, tab2_words, ta
         m1 = sb.tile([P, J], F32, name="m1")
         for h in range(2):
             nc.vector.scalar_tensor_tensor(m1[:, halves[h]], h1_sq[:, halves[h]], 1.0, ta_ps[h][:], ALU.subtract, ALU.mult)
-        wo_q = quantise("wo_q", wo_g)
-        product(c_ps[0][:], wo_q, dy_q0[0][:].bitcast(FP8X4), dy_q0[1][:])
-        m2 = sb.tile([P, J], F32, name="m2", tag="wo_raw", align_bytes=64)
+        wo_q = quantise("wo_q", wo_g, tag="dtab_wg1")
+        dy_q1 = quantise("dy_q1", dy_g1)
+        for h, dy_q in enumerate((dy_q0, dy_q1)):
+            product(c_ps[h][:], wo_q, dy_q[0][:].bitcast(FP8X4), dy_q[1][:])
+        m2 = sb.tile([P, J], F32, name="m2")
         for h in range(2):
             nc.vector.scalar_tensor_tensor(m2[:, halves[h]], th_sq[:, halves[h]], 0.25, m1[:, halves[h]], ALU.subtract, ALU.mult)
-        dy_q1 = quantise("dy_q1", dy_g1)
-        product(c_ps[1][:], wo_q, dy_q1[0][:].bitcast(FP8X4), dy_q1[1][:])
-        m3 = sb.tile([P, J], F32, name="m3", tag="dy_raw1", align_bytes=64)
+        m3 = sb.tile([P, J], F32, name="m3")
         for h in range(2):
             nc.vector.tensor_tensor(m3[:, halves[h]], m2[:, halves[h]], c_ps[h][:], ALU.mult)
-        res = sb.tile([P, J], F32, name="res", tag="dy_q1_codes", align_bytes=64)
+        res = sb.tile([P, J], F32, name="res")
         for h in range(2):
             nc.vector.scalar_tensor_tensor(res[:, halves[h]], m3[:, halves[h]], og_col[:], base_sb[:, halves[h]], ALU.mult, ALU.add)
             nc.sync.dma_start(out[:, halves[h]], res[:, halves[h]])

@@ -93,11 +93,11 @@ def tile_attend_hvtwotables_kernel(tc, tab_words, tab_scales, w1, tab2_words, ta
         w1_raw = load_rows("w1_raw", w1, 0, R)
         tab2_w = load_words("tab2_w", tab2_words)
         idx2 = load_list("idx2", offs2)
-        load_scale_rows(tab2_s, tab2_scales)
         w2_raw = load_rows("w2_raw", w2, 0, R)
+        load_scale_rows(tab2_s, tab2_scales)
         dy_raw0 = load_rows("dy_raw0", dy, 0, HALF)
-        load_scale_rows(dtab_s, dtab_scales)
         dtab_w = load_words("dtab_w", dtab_words)
+        load_scale_rows(dtab_s, dtab_scales)
         nc.sync.dma_start(bias_col[:], bias)
         wo_raw = load_rows("wo_raw", wo, 0, R)
         dy_raw1 = load_rows("dy_raw1", dy, HALF, HALF)
@@ -133,18 +133,19 @@ def tile_attend_hvtwotables_kernel(tc, tab_words, tab_scales, w1, tab2_words, ta
         nc.scalar.activation(th[:], b_ps[:], ACT.Tanh, bias=half_bias[:], scale=0.5)
         dy_g1 = interleave("dy_g1", dy_raw1)
         th_sq = sb.tile([P, J], F32, name="th_sq", tag="dy_raw1", align_bytes=64)
-        nc.scalar.activation(th_sq[:], th[:], ACT.Square, scale=0.5)
-
-        dtab_sg = gather("dtab_sg", dtab_s, idx[:], U8, tag="w2_raw")
         for h in range(2):
-            dtab_wg = gather("dtab_wg%d" % h, dtab_w, idx[:, h * LIST_COLS // 2:(h + 1) * LIST_COLS // 2], U16)
-            product(ta_ps[h][:], w1_q, dtab_wg[:].bitcast(FP4X4), dtab_sg[:, halves[h]])
+            nc.scalar.activation(th_sq[:, halves[h]], th[:, halves[h]], ACT.Square, scale=0.5)
 
-        dy_q0 = quantise("dy_q0", dy_g0, tag="dtab_wg0")
+        dtab_wg = gather("dtab_wg", dtab_w, idx[:], U16, tag="w2_raw")
+        for h in range(2):
+            dtab_sg = gather("dtab_sg%d" % h, dtab_s, idx[:, h * LIST_COLS // 2:(h + 1) * LIST_COLS // 2], U8)
+            product(ta_ps[h][:], w1_q, dtab_wg[:, halves[h]].bitcast(FP4X4), dtab_sg[:])
+
+        dy_q0 = quantise("dy_q0", dy_g0, tag="dtab_sg0")
         m1 = sb.tile([P, J], F32, name="m1")
         for h in range(2):
             nc.vector.scalar_tensor_tensor(m1[:, halves[h]], h1_sq[:, halves[h]], 1.0, ta_ps[h][:], ALU.subtract, ALU.mult)
-        wo_q = quantise("wo_q", wo_g, tag="dtab_wg1")
+        wo_q = quantise("wo_q", wo_g, tag="dtab_sg1")
         dy_q1 = quantise("dy_q1", dy_g1)
         for h, dy_q in enumerate((dy_q0, dy_q1)):
             product(c_ps[h][:], wo_q, dy_q[0][:].bitcast(FP8X4), dy_q[1][:])

from contextlib import ExitStack

import concourse.mybir as mybir

K, R, F, T, J = 512, 128, 512, 2048, 512
FLOPS = 4 * 2 * K * R * J

F32 = mybir.dt.float32
BF16 = mybir.dt.bfloat16
I32 = mybir.dt.int32
U32 = mybir.dt.uint32
U16 = mybir.dt.uint16
U8 = mybir.dt.uint8
FP8X4 = mybir.dt.float8_e4m3fn_x4
FP4X4 = mybir.dt.float4_e2m1fn_x4
ALU = mybir.AluOpType
ACT = mybir.ActivationFunctionType

P = 128
PACK = 4
HALF = J // 2
LIST_COLS = J // 16


def tile_attend_hvtwotables_kernel(tc, tab_words, tab_scales, w1, tab2_words, tab2_scales, w2, bias, wo, dy,
                                    dtab_words, dtab_scales, og, base, offs, offs2, out):
    nc = tc.nc
    with ExitStack() as ctx:
        sb = ctx.enter_context(tc.tile_pool(name="sb", bufs=1))
        ps = ctx.enter_context(tc.psum_pool(name="ps", bufs=1))

        def zeroed_scale_table(name):
            table = sb.tile([P, T], U8, name=name, tag=name, align_bytes=64)
            nc.vector.memset(table[:].bitcast(I32), 0)
            return table

        def load_scale_rows(table, scales):
            rows = scales[0].bitcast(I32)
            for r in range(4):
                nc.sync.dma_start(table[:].bitcast(I32)[r:P:32, :], rows[r:16:4, :])

        def load_words(name, words):
            table = sb.tile([P, T], U16, name=name, tag=name, align_bytes=64)
            nc.sync.dma_start(table[:].bitcast(I32), words[0].bitcast(I32))
            return table

        def load_list(name, src):
            lst = sb.tile([P, LIST_COLS], U16, name=name)
            nc.sync.dma_start(lst[:], src)
            return lst

        def load_rows(name, src, c0, width):
            raw = sb.tile([P, PACK, width], F32, name=name, tag=name, align_bytes=64)
            nc.sync.dma_start(raw[:], src.rearrange("(p t) c -> p t c", t=PACK)[:, :, c0:c0 + width])
            return raw

        def interleave(name, raw, tag=None):
            grouped = sb.tile([P, raw.shape[2], PACK], BF16, name=name, tag=tag or name, align_bytes=64)
            nc.scalar.activation(
                grouped[:].rearrange("p (c i) t -> p c t i", i=4),
                raw[:].rearrange("p t (c i) -> p c t i", i=4),
                ACT.Copy,
            )
            return grouped

        def quantise(name, grouped, tag=None):
            width = grouped.shape[1]
            codes = sb.tile([P, width], U32, name=name + "_codes", tag=tag or name + "_codes", align_bytes=64)
            scales = sb.tile([P, width], U8, name=name + "_scales", align_bytes=64)
            nc.vector.quantize_mx(codes[:].bitcast(FP8X4), scales[:], grouped[:].rearrange("p c t -> p (c t)"))
            return codes, scales

        def gather(name, table, offsets, dtype, tag=None):
            picked = sb.tile([P, offsets.shape[1] * 16], dtype, name=name, tag=tag or name, align_bytes=64)
            nc.vector.tensor_copy(picked[:], table[:].indirect(offsets))
            return picked

        def product(acc, weights, codes, scales):
            nc.tensor.matmul_mx(acc, lhsT=weights[0][:].bitcast(FP8X4), lhsT_scale=weights[1][:],
                                rhs=codes, rhs_scale=scales, start=True, stop=True)

        tab_s = zeroed_scale_table("tab_s")
        tab2_s = zeroed_scale_table("tab2_s")
        dtab_s = zeroed_scale_table("dtab_s")

        bias_col = sb.tile([P, 1], F32, name="bias_col")
        og_col = sb.tile([P, 1], F32, name="og_col")
        base_sb = sb.tile([P, J], F32, name="base_sb")

        tab_w = load_words("tab_w", tab_words)
        idx = load_list("idx", offs)
        load_scale_rows(tab_s, tab_scales)
        w1_raw = load_rows("w1_raw", w1, 0, R)
        tab2_w = load_words("tab2_w", tab2_words)
        idx2 = load_list("idx2", offs2)
        w2_raw = load_rows("w2_raw", w2, 0, R)
        load_scale_rows(tab2_s, tab2_scales)
        dy_raw0 = load_rows("dy_raw0", dy, 0, HALF)
        dtab_w = load_words("dtab_w", dtab_words)
        load_scale_rows(dtab_s, dtab_scales)
        nc.sync.dma_start(bias_col[:], bias)
        wo_raw = load_rows("wo_raw", wo, 0, R)
        dy_raw1 = load_rows("dy_raw1", dy, HALF, HALF)
        nc.sync.dma_start(og_col[:], og)
        nc.sync.dma_start(base_sb[:], base)

        a_ps = ps.tile([P, J], F32, name="a_ps")
        b_ps = ps.tile([P, J], F32, name="b_ps")
        c_ps = [ps.tile([P, HALF], F32, name="c_ps%d" % h) for h in range(2)]
        ta_ps = [ps.tile([P, HALF], F32, name="ta_ps%d" % h) for h in range(2)]
        halves = [slice(h * HALF, (h + 1) * HALF) for h in range(2)]

        tab_wg = gather("tab_wg", tab_w, idx[:], U16)
        tab_sg = gather("tab_sg", tab_s, idx[:], U8)
        w1_q = quantise("w1_q", interleave("w1_g", w1_raw))
        product(a_ps[:], w1_q, tab_wg[:].bitcast(FP4X4), tab_sg[:])

        tab2_wg = gather("tab2_wg", tab2_w, idx2[:], U16, tag="w1_raw")
        tab2_sg = gather("tab2_sg", tab2_s, idx2[:], U8)
        w2_q = quantise("w2_q", interleave("w2_g", w2_raw))
        product(b_ps[:], w2_q, tab2_wg[:].bitcast(FP4X4), tab2_sg[:])

        h1 = sb.tile([P, J], F32, name="h1")
        nc.scalar.activation(h1[:], a_ps[:], ACT.Tanh)
        h1_sq = sb.tile([P, J], F32, name="h1_sq")
        nc.scalar.activation(h1_sq[:], h1[:], ACT.Square)

        dy_g0 = interleave("dy_g0", dy_raw0)
        wo_g = interleave("wo_g", wo_raw)
        half_bias = sb.tile([P, 1], F32, name="half_bias")
        nc.scalar.activation(half_bias[:], bias_col[:], ACT.Copy, scale=0.5)
        th = sb.tile([P, J], F32, name="th", tag="wo_raw", align_bytes=64)
        nc.scalar.activation(th[:], b_ps[:], ACT.Tanh, bias=half_bias[:], scale=0.5)
        dy_g1 = interleave("dy_g1", dy_raw1)
        th_sq = sb.tile([P, J], F32, name="th_sq", tag="dy_raw1", align_bytes=64)
        for h in range(2):
            nc.scalar.activation(th_sq[:, halves[h]], th[:, halves[h]], ACT.Square, scale=0.5)

        dtab_wg = gather("dtab_wg", dtab_w, idx[:], U16, tag="w2_raw")
        for h in range(2):
            dtab_sg = gather("dtab_sg%d" % h, dtab_s, idx[:, h * LIST_COLS // 2:(h + 1) * LIST_COLS // 2], U8)
            product(ta_ps[h][:], w1_q, dtab_wg[:, halves[h]].bitcast(FP4X4), dtab_sg[:])

        dy_q0 = quantise("dy_q0", dy_g0, tag="dtab_sg0")
        m1 = sb.tile([P, J], F32, name="m1")
        for h in range(2):
            nc.vector.scalar_tensor_tensor(m1[:, halves[h]], h1_sq[:, halves[h]], 1.0, ta_ps[h][:], ALU.subtract, ALU.mult)
        wo_q = quantise("wo_q", wo_g, tag="dtab_sg1")
        dy_q1 = quantise("dy_q1", dy_g1)
        for h, dy_q in enumerate((dy_q0, dy_q1)):
            product(c_ps[h][:], wo_q, dy_q[0][:].bitcast(FP8X4), dy_q[1][:])
        m2 = sb.tile([P, J], F32, name="m2")
        for h in range(2):
            nc.vector.scalar_tensor_tensor(m2[:, halves[h]], th_sq[:, halves[h]], 0.25, m1[:, halves[h]], ALU.subtract, ALU.mult)
        m3 = sb.tile([P, J], F32, name="m3")
        for h in range(2):
            nc.vector.tensor_tensor(m3[:, halves[h]], m2[:, halves[h]], c_ps[h][:], ALU.mult)
        res = sb.tile([P, J], F32, name="res")
        for h in range(2):
            nc.vector.scalar_tensor_tensor(res[:, halves[h]], m3[:, halves[h]], og_col[:], base_sb[:, halves[h]], ALU.mult, ALU.add)
            nc.sync.dma_start(out[:, halves[h]], res[:, halves[h]])
